import numpy as np
import ml_dtypes


def mxq(x, axis, fmt="e4m3"):
    dtype, down = {"e4m3": (ml_dtypes.float8_e4m3fn, 7), "e5m2": (ml_dtypes.float8_e5m2, 14)}[fmt]
    v = np.moveaxis(np.asarray(x, np.float32).astype(ml_dtypes.bfloat16).astype(np.float64), axis, -1)
    blocks = v.reshape(v.shape[:-1] + (-1, 32))
    amax = np.abs(blocks).max(-1, keepdims=True)
    byte = np.maximum(np.where(amax > 0, np.frexp(amax)[1] - 1 + 127, 0) - down, 1)
    scale = np.exp2(byte - 127.0)
    codes = (blocks / scale).astype(np.float32).astype(dtype).astype(np.float64)
    return np.moveaxis((codes * scale).reshape(v.shape), -1, axis)


WIDE = False


def mx_kscale(k):
    if not WIDE:
        return np.ones(k)
    levels = np.array([30, -30])
    if k % 512:
        return np.exp2(np.random.permutation(np.resize(levels, k // 32))).repeat(32)
    a = np.empty((k // 512, 16))
    for p in range(k // 512):
        a[p, :8] = np.random.permutation(np.resize(levels, 8))
        for g in range(8):
            far = levels[np.abs(levels - a[p, g]) >= 10]
            a[p, g + 8] = far[np.random.randint(len(far))]
    return np.exp2(a.ravel()).repeat(32)


def f64(x):
    return np.asarray(x).astype(np.float64)


def striped(idx):
    return np.tile(np.asarray(idx).reshape(-1, 16).T, (8, 1)).astype(np.uint16)


def unstriped(offs):
    return offs[:16].T.reshape(-1).astype(np.int64)


E2M1 = np.array([0.0, 0.5, 1.0, 1.5, 2.0, 3.0, 4.0, 6.0, -0.0, -0.5, -1.0, -1.5, -2.0, -3.0, -4.0, -6.0])


def pack_weight(w, fmt):
    k, n = w.shape
    w = f64(np.asarray(w, np.float32).astype(ml_dtypes.bfloat16)).reshape(k // 32, 32, n)
    amax = np.abs(w).max(1)
    if fmt in ("e4m3", "e5m2"):
        byte = np.frexp(amax)[1] - 1 + 127 - (7 if fmt == "e4m3" else 14)
    else:
        mant, ex = np.frexp(amax / 6.0)
        byte = np.where(mant > 0.5, ex, ex - 1) + 127
    byte = np.clip(np.where(amax > 0, byte, 1), 1, 254)
    scaled = (w * np.exp2(127.0 - byte)[:, None, :]).reshape(k, n).astype(np.float32)
    by_word = np.ascontiguousarray(scaled.reshape(k // 512, 128, 4, n).transpose(0, 1, 3, 2))
    if fmt in ("e4m3", "e5m2"):
        words = by_word.astype(ml_dtypes.float8_e4m3fn if fmt == "e4m3" else ml_dtypes.float8_e5m2).view(np.uint8)
    else:
        c = by_word.astype(ml_dtypes.float4_e2m1fn).view(np.uint8) & 0xF
        words = (c[..., 0::2] | (c[..., 1::2] << 4)).reshape(k // 512, 128, 2 * n)
    return np.ascontiguousarray(words), np.ascontiguousarray(byte.astype(np.uint8).reshape(k // 512, 16, n))


def unpack_weight(words, scales, fmt):
    g, _, n = scales.shape
    words = np.ascontiguousarray(words).reshape(g, 128, n, -1)
    if fmt in ("e4m3", "e5m2"):
        vals = words.view(ml_dtypes.float8_e4m3fn if fmt == "e4m3" else ml_dtypes.float8_e5m2).astype(np.float64)
    else:
        nib = np.empty((g, 128, n, 4), np.uint8)
        nib[..., 0::2] = words & 0xF
        nib[..., 1::2] = words >> 4
        vals = E2M1[nib]
    vals = vals * np.repeat(np.exp2(scales.astype(np.float64) - 127.0), 8, axis=1)[..., None]
    return vals.transpose(0, 1, 3, 2).reshape(g * 512, n)


K, T, Z, J, R, N, C, O = 512, 1024, 1024, 256, 512, 256, 512, 128


def setup_inputs():
    n = np.random.standard_normal
    idx = np.random.permutation(T)[:J]
    idx2 = np.random.permutation(Z)[:J]
    idx3 = np.random.permutation(C)[:J]
    idx4 = np.random.permutation(C)[:J]
    idx5 = np.random.permutation(J)[:O]
    idx6 = np.random.permutation(J)[:O]
    fk = mx_kscale(K)
    fr = mx_kscale(R)
    xtp = pack_weight(n((K, T)) / fk[:, None], "e4m3")
    xop = pack_weight(n((K, Z)) / fk[:, None], "e2m1")
    wp = pack_weight(n((K, R)) * 1 / np.sqrt(K) * fk[:, None] * fr, "e5m2")
    w2p = pack_weight(n((K, R)) * 1 / np.sqrt(K) * fk[:, None] * fr, "e5m2")
    wbp = pack_weight(n((R, N)) * 1 / np.sqrt(R) / fr[:, None], "e5m2")
    wcp = pack_weight(n((R, N)) * 1 / np.sqrt(R) / fr[:, None], "e2m1")
    return {
        "xt_words": xtp[0],
        "xt_scales": xtp[1],
        "xo_words": xop[0],
        "xo_scales": xop[1],
        "w_words": wp[0],
        "w_scales": wp[1],
        "w2_words": w2p[0],
        "w2_scales": w2p[1],
        "wb_words": wbp[0],
        "wb_scales": wbp[1],
        "wc_words": wcp[0],
        "wc_scales": wcp[1],
        "so": (np.random.uniform(0.5, 1.6, (N, 1))).astype(np.float32),
        "sp": (np.random.uniform(0.5, 1.6, (N, 1))).astype(np.float32),
        "offs": striped(idx),
        "offs2": striped(idx2),
        "offs3": striped(idx3),
        "offs4": striped(idx4),
        "offs5": striped(idx5),
        "offs6": striped(idx6),
    }


def reference(xt_words, xt_scales, xo_words, xo_scales, w_words, w_scales, w2_words, w2_scales, wb_words, wb_scales, wc_words, wc_scales, so, sp, offs, offs2, offs3, offs4, offs5, offs6):
    idx = unstriped(offs)
    idx2 = unstriped(offs2)
    idx3 = unstriped(offs3)
    idx4 = unstriped(offs4)
    idx5 = unstriped(offs5)
    idx6 = unstriped(offs6)
    xtu = unpack_weight(xt_words, xt_scales, "e4m3")
    xou = unpack_weight(xo_words, xo_scales, "e2m1")
    wu = unpack_weight(w_words, w_scales, "e5m2")
    w2u = unpack_weight(w2_words, w2_scales, "e5m2")
    wbu = unpack_weight(wb_words, wb_scales, "e5m2")
    wcu = unpack_weight(wc_words, wc_scales, "e2m1")
    xtidxg = xtu[:, idx]
    xoidx2g = xou[:, idx2]
    a = wu.T @ xtidxg + w2u.T @ xoidx2g
    b = w2u.T @ xtidxg + wu.T @ xoidx2g
    hid = np.maximum(a, b)
    hidq = mxq(hid, 0, "e4m3")
    p = wbu.T @ hidq
    q = wcu.T @ hidq
    pw = np.zeros((N, C))
    pw[:, idx3] = p
    m0 = np.maximum(pw[:, idx4] * f64(so), q)
    y = m0[:, idx5] - m0[:, idx6] * f64(sp)
    return y

@@ -1,0 +1,209 @@
+from contextlib import ExitStack
+
+import concourse.mybir as mybir
+
+K, T, Z, J, R, N, C, O = 512, 1024, 1024, 256, 512, 256, 512, 128
+FLOPS = 2 * (4 * K * R * J + 2 * R * N * J)
+
+F32 = mybir.dt.float32
+BF16 = mybir.dt.bfloat16
+I32 = mybir.dt.int32
+U32 = mybir.dt.uint32
+U16 = mybir.dt.uint16
+U8 = mybir.dt.uint8
+E4M3 = mybir.dt.float8_e4m3fn_x4
+E5M2 = mybir.dt.float8_e5m2_x4
+E2M1 = mybir.dt.float4_e2m1fn_x4
+COPY = mybir.ActivationFunctionType.Copy
+MAX = mybir.AluOpType.max
+SUB = mybir.AluOpType.subtract
+
+P = 128
+PACK = 4
+H = 2
+JH = J // H
+NT = N // P
+
+
+def tile_list_outcomechain_crossed_kernel(
+    tc, xt_words, xt_scales, xo_words, xo_scales, w_words, w_scales, w2_words, w2_scales,
+    wb_words, wb_scales, wc_words, wc_scales, so, sp, offs, offs2, offs3, offs4, offs5, offs6, out,
+):
+    nc = tc.nc
+    with ExitStack() as ctx:
+        lists = ctx.enter_context(tc.tile_pool(name="lists", bufs=1))
+        sb = ctx.enter_context(tc.tile_pool(name="sb", bufs=1))
+        ps = ctx.enter_context(tc.psum_pool(name="ps", bufs=1))
+
+        def tile(name, shape, dtype):
+            return sb.tile(shape, dtype, name=name, align_bytes=64)
+
+        def load_list(name, src):
+            t = lists.tile(list(src.shape), U16, name=name)
+            nc.sync.dma_start(t[:], src)
+            return t
+
+        def words32(src):
+            return src[0].rearrange("p n t -> p (n t)").bitcast(I32)
+
+        xo_s = tile("xo_s", [P, Z // 4], I32)
+        xt_s = tile("xt_s", [P, T // 4], I32)
+        w_st = tile("w_st", [4, 4, R // 4], I32)
+        w_s = tile("w_s", [P, R // 4], I32)
+        w2_s = tile("w2_s", [P, 4, R // 4], I32)
+        o_s = tile("o_s", [P, 4, 2, N // 4], I32)
+        nc.vector.memset(xo_s[:], 0)
+        nc.vector.memset(w_s[:], 0)
+        nc.vector.memset(w2_s[:, 0, :], 0)
+        nc.vector.memset(xt_s[:], 0)
+        nc.vector.memset(o_s[:, 0, :, :], 0)
+        pw = [tile(f"pw{t}", [P, C], F32) for t in range(NT)]
+        for t in range(NT):
+            nc.vector.memset(pw[t][:], 0.0)
+
+        xo_w = tile("xo_w", [P, Z], U16)
+        xt_w = tile("xt_w", [P, T], U32)
+        w_w = tile("w_w", [P, R], U32)
+        w2_w = tile("w2_w", [P, R], U32)
+        wb_w = tile("wb_w", [P, N], U32)
+        wc_w = tile("wc_w", [P, 2 * N], U8)
+        so_t = tile("so_t", [P, NT], F32)
+        sp_t = tile("sp_t", [P, NT], F32)
+
+        def load_rows(plane, src):
+            for q in range(4):
+                nc.sync.dma_start(plane[32 * q : 32 * q + 4, :], src[0, 4 * q : 4 * q + 4, :].bitcast(I32))
+
+        def load_staged(dst, src):
+            nc.sync.dma_start(dst, src[0].rearrange("(q r) n -> r q n", r=4).bitcast(I32))
+
+        load_staged(w_st[:], w_scales)
+        l2 = load_list("l2", offs2)
+        nc.sync.dma_start(xo_w[:].bitcast(I32), xo_words[0].bitcast(I32))
+        nc.sync.dma_start(w_w[:].bitcast(I32), words32(w_words))
+        load_rows(xo_s, xo_scales)
+        load_staged(w2_s[0:4, :, :], w2_scales)
+        nc.sync.dma_start(w2_w[:].bitcast(I32), words32(w2_words))
+        nc.sync.dma_start(xt_w[:].bitcast(I32), words32(xt_words))
+        l1 = load_list("l1", offs)
+        load_rows(xt_s, xt_scales)
+        load_staged(o_s[0:4, :, 0, :], wb_scales)
+        load_staged(o_s[0:4, :, 1, :], wc_scales)
+        nc.sync.dma_start(wb_w[:].bitcast(I32), words32(wb_words))
+        nc.sync.dma_start(wc_w[:].bitcast(I32), wc_words[0].bitcast(I32))
+        l3 = load_list("l3", offs3)
+        l4 = load_list("l4", offs4)
+        with nc.allow_non_contiguous_dma(reason="one value a partition"):
+            nc.gpsimd.dma_start(so_t[:], so.rearrange("(t p) o -> p (t o)", p=P))
+            nc.gpsimd.dma_start(sp_t[:], sp.rearrange("(t p) o -> p (t o)", p=P))
+        l6 = load_list("l6", offs6)
+        l5 = load_list("l5", offs5)
+
+
+        def deal(engine_copy, dst, src):
+            engine_copy(dst.rearrange("p (t m) -> p m t", t=PACK), src.rearrange("p (m t) -> p m t", t=PACK))
+
+        def half(lst, h):
+            cols = JH // 16
+            return lst[:, h * cols : (h + 1) * cols]
+
+        def gather_half(name, window, lst, h, dtype):
+            g = tile(f"{name}{h}", [P, JH], dtype)
+            nc.vector.tensor_copy(g[:], window.indirect(half(lst, h)))
+            return g
+
+        w_d = tile("w_d", [P, R], U32)
+        w2_d = tile("w2_d", [P, R], U32)
+        w_sd = tile("w_sd", [P, R], U8)
+        w2_sd = tile("w2_sd", [P, R], U8)
+        deal(nc.scalar.copy, w_d[:], w_w[:])
+        deal(nc.scalar.copy, w2_d[:], w2_w[:])
+
+        gxo_s, gxo_w, gxt_s, gxt_w = [], [], [], []
+        for q in range(4):
+            nc.vector.tensor_copy(w_s[32 * q : 32 * q + 4, :], w_st[:, q, :])
+        deal(nc.vector.tensor_copy, w_sd[:], w_s[:].bitcast(U8))
+        for h in range(H):
+            gxo_w.append(gather_half("gxo_w", xo_w[:], l2, h, U16))
+            gxo_s.append(gather_half("gxo_s", xo_s[:].bitcast(U8), l2, h, U8))
+        for q in range(1, 4):
+            nc.vector.tensor_copy(w2_s[32 * q : 32 * q + 4, 0, :], w2_s[0:4, q, :])
+        deal(nc.vector.tensor_copy, w2_sd[:], w2_s[:, 0, :].bitcast(U8))
+        for h in range(H):
+            gxt_w.append(gather_half("gxt_w", xt_w[:], l1, h, U32))
+            gxt_s.append(gather_half("gxt_s", xt_s[:].bitcast(U8), l1, h, U8))
+        for q in range(1, 4):
+            nc.vector.tensor_copy(o_s[32 * q : 32 * q + 4, 0, :, :], o_s[0:4, q, :, :])
+
+        a_ps = [ps.tile([P, PACK, JH], F32, name=f"a{h}") for h in range(H)]
+        b_ps = [ps.tile([P, PACK, JH], F32, name=f"b{h}") for h in range(H)]
+
+        def passes(bank, words, scales, x_words, x_scales, first):
+            for t in range(PACK):
+                cols = slice(t * P, (t + 1) * P)
+                nc.tensor.matmul_mx(
+                    bank[:, t, :], lhsT=words[:, cols].bitcast(E5M2), lhsT_scale=scales[:, cols],
+                    rhs=x_words, rhs_scale=x_scales,
+                    start=first and t == 0, stop=(not first) and t == PACK - 1,
+                )
+
+        for h in range(H):
+            passes(b_ps[h], w_d, w_sd, gxo_w[h][:].bitcast(E2M1), gxo_s[h][:], True)
+        for h in range(H):
+            passes(a_ps[h], w2_d, w2_sd, gxo_w[h][:].bitcast(E2M1), gxo_s[h][:], True)
+        for h in range(H):
+            passes(a_ps[h], w_d, w_sd, gxt_w[h][:].bitcast(E4M3), gxt_s[h][:], False)
+            passes(b_ps[h], w2_d, w2_sd, gxt_w[h][:].bitcast(E4M3), gxt_s[h][:], False)
+
+        wb_s = o_s[:, 0, 0, :].bitcast(U8)
+        wc_s = o_s[:, 0, 1, :].bitcast(U8)
+        q_ps = ps.tile([P, NT, J], F32, name="q")
+        p_ps = [ps.tile([P, J], F32, name=f"p{t}") for t in range(NT)]
+        JQ = JH // 2
+        hq, hs = [], []
+        for h in range(H):
+            hid = tile(f"hid{h}", [P, JH, PACK], BF16)
+            for u in range(2):
+                js = slice(u * JQ, (u + 1) * JQ)
+                a_sb = tile(f"a_sb{h}{u}", [P, JQ, PACK], F32)
+                nc.scalar.activation(a_sb[:], a_ps[h][:, :, js].rearrange("p t j -> p j t"), COPY)
+                nc.vector.tensor_tensor(hid[:, js, :], b_ps[h][:, :, js].rearrange("p t j -> p j t"), a_sb[:], MAX)
+            hq.append(tile(f"hq{h}", [P, JH], U32))
+            hs.append(tile(f"hs{h}", [P, JH], U8))
+            nc.vector.quantize_mx(hq[h][:].bitcast(E4M3), hs[h][:], hid[:].rearrange("p j t -> p (j t)"))
+        for h in range(H):
+            for t in range(NT):
+                cols = slice(t * P, (t + 1) * P)
+                nc.tensor.matmul_mx(
+                    p_ps[t][:, h * JH : (h + 1) * JH], lhsT=wb_w[:, cols].bitcast(E5M2), lhsT_scale=wb_s[:, cols],
+                    rhs=hq[h][:].bitcast(E4M3), rhs_scale=hs[h][:], start=True, stop=True,
+                )
+        for h in range(H):
+            for t in range(NT):
+                cols = slice(t * P, (t + 1) * P)
+                nc.tensor.matmul_mx(
+                    q_ps[:, t, h * JH : (h + 1) * JH],
+                    lhsT=wc_w[:, 2 * t * P : 2 * (t + 1) * P].bitcast(E2M1), lhsT_scale=wc_s[:, cols],
+                    rhs=hq[h][:].bitcast(E4M3), rhs_scale=hs[h][:], start=True, stop=True,
+                )
+        p_sb = [tile(f"p_sb{t}", [P, J], F32) for t in range(NT)]
+        nc.scalar.copy(p_sb[0][:], p_ps[0][:])
+        nc.vector.tensor_copy(p_sb[1][:], p_ps[1][:])
+        nc.vector.tensor_copy(pw[0][:].indirect(l3[:]), p_sb[0][:])
+        nc.scalar.activation(pw[1][:].indirect(l3[:]), p_sb[1][:], COPY)
+
+        m0 = [tile(f"m0{t}", [P, J], F32) for t in range(NT)]
+        g5 = [tile(f"g5{t}", [P, O], F32) for t in range(NT)]
+        for t in range(NT):
+            for h in range(H):
+                js = slice(h * JH, (h + 1) * JH)
+                g4 = tile(f"g4{t}{h}", [P, JH], F32)
+                nc.scalar.activation(g4[:], pw[t][:].indirect(half(l4, h)), COPY, scale=so_t[:, t : t + 1])
+                nc.vector.tensor_tensor(m0[t][:, js], q_ps[:, t, js], g4[:], MAX)
+            nc.vector.tensor_copy(g5[t][:], m0[t][:].indirect(l5[:]))
+        for t in range(NT):
+            g6 = tile(f"g6{t}", [P, O], F32)
+            nc.scalar.activation(g6[:], m0[t][:].indirect(l6[:]), COPY, scale=sp_t[:, t : t + 1])
+            y = tile(f"y{t}", [P, O], F32)
+            nc.vector.tensor_tensor(y[:], g5[t][:], g6[:], SUB)
+            nc.sync.dma_start(out[t * P : (t + 1) * P, :], y[:])

@@ -35,8 +35,8 @@ def tile_list_outcomechain_crossed_kernel(
         sb = ctx.enter_context(tc.tile_pool(name="sb", bufs=1))
         ps = ctx.enter_context(tc.psum_pool(name="ps", bufs=1))
 
-        def tile(name, shape, dtype):
-            return sb.tile(shape, dtype, name=name, align_bytes=64)
+        def tile(name, shape, dtype, tag=None):
+            return sb.tile(shape, dtype, name=name, tag=tag or name, align_bytes=64)
 
         def load_list(name, src):
             t = lists.tile(list(src.shape), U16, name=name)
@@ -51,12 +51,14 @@ def tile_list_outcomechain_crossed_kernel(
         w_st = tile("w_st", [4, 4, R // 4], I32)
         w_s = tile("w_s", [P, R // 4], I32)
         w2_s = tile("w2_s", [P, 4, R // 4], I32)
-        o_s = tile("o_s", [P, 4, 2, N // 4], I32)
-        nc.vector.memset(xo_s[:], 0)
+        wb_s = tile("wb_s", [P, N // 4], I32)
+        wc_s = tile("wc_s", [P, N // 4], I32)
+        nc.vector.memset(xt_s[:], 0)
         nc.vector.memset(w_s[:], 0)
         nc.vector.memset(w2_s[:, 0, :], 0)
-        nc.vector.memset(xt_s[:], 0)
-        nc.vector.memset(o_s[:, 0, :, :], 0)
+        nc.vector.memset(xo_s[:], 0)
+        nc.vector.memset(wb_s[:], 0)
+        nc.vector.memset(wc_s[:], 0)
         pw = [tile(f"pw{t}", [P, C], F32) for t in range(NT)]
         for t in range(NT):
             nc.vector.memset(pw[t][:], 0.0)
@@ -78,30 +80,35 @@ def tile_list_outcomechain_crossed_kernel(
             nc.sync.dma_start(dst, src[0].rearrange("(q r) n -> r q n", r=4).bitcast(I32))
 
         load_staged(w_st[:], w_scales)
-        l2 = load_list("l2", offs2)
-        nc.sync.dma_start(xo_w[:].bitcast(I32), xo_words[0].bitcast(I32))
+        l1 = load_list("l1", offs)
+        nc.sync.dma_start(xt_w[:].bitcast(I32), words32(xt_words))
         nc.sync.dma_start(w_w[:].bitcast(I32), words32(w_words))
-        load_rows(xo_s, xo_scales)
+        load_rows(xt_s, xt_scales)
         load_staged(w2_s[0:4, :, :], w2_scales)
         nc.sync.dma_start(w2_w[:].bitcast(I32), words32(w2_words))
-        nc.sync.dma_start(xt_w[:].bitcast(I32), words32(xt_words))
-        l1 = load_list("l1", offs)
-        load_rows(xt_s, xt_scales)
-        load_staged(o_s[0:4, :, 0, :], wb_scales)
-        load_staged(o_s[0:4, :, 1, :], wc_scales)
+        nc.sync.dma_start(xo_w[:].bitcast(I32), xo_words[0].bitcast(I32))
+        l2 = load_list("l2", offs2)
+        load_rows(xo_s, xo_scales)
+        load_rows(wb_s, wb_scales)
         nc.sync.dma_start(wb_w[:].bitcast(I32), words32(wb_words))
-        nc.sync.dma_start(wc_w[:].bitcast(I32), wc_words[0].bitcast(I32))
         l3 = load_list("l3", offs3)
+        nc.sync.dma_start(wc_w[:].bitcast(I32), wc_words[0].bitcast(I32))
+        load_rows(wc_s, wc_scales)
         l4 = load_list("l4", offs4)
         with nc.allow_non_contiguous_dma(reason="one value a partition"):
-            nc.gpsimd.dma_start(so_t[:], so.rearrange("(t p) o -> p (t o)", p=P))
-            nc.gpsimd.dma_start(sp_t[:], sp.rearrange("(t p) o -> p (t o)", p=P))
+            nc.sync.dma_start(so_t[:], so.rearrange("(t p) o -> p (t o)", p=P))
+            nc.sync.dma_start(sp_t[:], sp.rearrange("(t p) o -> p (t o)", p=P))
         l6 = load_list("l6", offs6)
         l5 = load_list("l5", offs5)
 
 
-        def deal(engine_copy, dst, src):
-            engine_copy(dst.rearrange("p (t m) -> p m t", t=PACK), src.rearrange("p (m t) -> p m t", t=PACK))
+        def deal_words(dst, src):
+            nc.scalar.copy(
+                dst.rearrange("p (t m i) -> p m t i", t=PACK, i=4), src.rearrange("p (m i t) -> p m t i", t=PACK, i=4)
+            )
+
+        def deal_bytes(dst, src):
+            nc.vector.tensor_copy(dst.rearrange("p (t m) -> p t m", t=PACK), src.rearrange("p (m t) -> p t m", t=PACK))
 
         def half(lst, h):
             cols = JH // 16
@@ -116,24 +123,22 @@ def tile_list_outcomechain_crossed_kernel(
         w2_d = tile("w2_d", [P, R], U32)
         w_sd = tile("w_sd", [P, R], U8)
         w2_sd = tile("w2_sd", [P, R], U8)
-        deal(nc.scalar.copy, w_d[:], w_w[:])
-        deal(nc.scalar.copy, w2_d[:], w2_w[:])
+        deal_words(w_d[:], w_w[:])
+        deal_words(w2_d[:], w2_w[:])
 
         gxo_s, gxo_w, gxt_s, gxt_w = [], [], [], []
         for q in range(4):
             nc.vector.tensor_copy(w_s[32 * q : 32 * q + 4, :], w_st[:, q, :])
-        deal(nc.vector.tensor_copy, w_sd[:], w_s[:].bitcast(U8))
-        for h in range(H):
-            gxo_w.append(gather_half("gxo_w", xo_w[:], l2, h, U16))
-            gxo_s.append(gather_half("gxo_s", xo_s[:].bitcast(U8), l2, h, U8))
-        for q in range(1, 4):
-            nc.vector.tensor_copy(w2_s[32 * q : 32 * q + 4, 0, :], w2_s[0:4, q, :])
-        deal(nc.vector.tensor_copy, w2_sd[:], w2_s[:, 0, :].bitcast(U8))
+        deal_bytes(w_sd[:], w_s[:].bitcast(U8))
         for h in range(H):
             gxt_w.append(gather_half("gxt_w", xt_w[:], l1, h, U32))
             gxt_s.append(gather_half("gxt_s", xt_s[:].bitcast(U8), l1, h, U8))
         for q in range(1, 4):
-            nc.vector.tensor_copy(o_s[32 * q : 32 * q + 4, 0, :, :], o_s[0:4, q, :, :])
+            nc.vector.tensor_copy(w2_s[32 * q : 32 * q + 4, 0, :], w2_s[0:4, q, :])
+        deal_bytes(w2_sd[:], w2_s[:, 0, :].bitcast(U8))
+        for h in range(H):
+            gxo_w.append(gather_half("gxo_w", xo_w[:], l2, h, U16))
+            gxo_s.append(gather_half("gxo_s", xo_s[:].bitcast(U8), l2, h, U8))
 
         a_ps = [ps.tile([P, PACK, JH], F32, name=f"a{h}") for h in range(H)]
         b_ps = [ps.tile([P, PACK, JH], F32, name=f"b{h}") for h in range(H)]
@@ -148,17 +153,14 @@ def tile_list_outcomechain_crossed_kernel(
                 )
 
         for h in range(H):
-            passes(b_ps[h], w_d, w_sd, gxo_w[h][:].bitcast(E2M1), gxo_s[h][:], True)
+            passes(a_ps[h], w_d, w_sd, gxt_w[h][:].bitcast(E4M3), gxt_s[h][:], True)
         for h in range(H):
-            passes(a_ps[h], w2_d, w2_sd, gxo_w[h][:].bitcast(E2M1), gxo_s[h][:], True)
+            passes(b_ps[h], w2_d, w2_sd, gxt_w[h][:].bitcast(E4M3), gxt_s[h][:], True)
         for h in range(H):
-            passes(a_ps[h], w_d, w_sd, gxt_w[h][:].bitcast(E4M3), gxt_s[h][:], False)
-            passes(b_ps[h], w2_d, w2_sd, gxt_w[h][:].bitcast(E4M3), gxt_s[h][:], False)
+            passes(a_ps[h], w2_d, w2_sd, gxo_w[h][:].bitcast(E2M1), gxo_s[h][:], False)
+            passes(b_ps[h], w_d, w_sd, gxo_w[h][:].bitcast(E2M1), gxo_s[h][:], False)
 
-        wb_s = o_s[:, 0, 0, :].bitcast(U8)
-        wc_s = o_s[:, 0, 1, :].bitcast(U8)
         q_ps = ps.tile([P, NT, J], F32, name="q")
-        p_ps = [ps.tile([P, J], F32, name=f"p{t}") for t in range(NT)]
         JQ = JH // 2
         hq, hs = [], []
         for h in range(H):
@@ -171,11 +173,13 @@ def tile_list_outcomechain_crossed_kernel(
             hq.append(tile(f"hq{h}", [P, JH], U32))
             hs.append(tile(f"hs{h}", [P, JH], U8))
             nc.vector.quantize_mx(hq[h][:].bitcast(E4M3), hs[h][:], hid[:].rearrange("p j t -> p (j t)"))
+        p_ps = {}
         for h in range(H):
             for t in range(NT):
                 cols = slice(t * P, (t + 1) * P)
+                p_ps[h, t] = ps.tile([P, JH], F32, name=f"p{h}{t}", tag="a0" if (h, t) == (1, 1) else f"p{h}{t}")
                 nc.tensor.matmul_mx(
-                    p_ps[t][:, h * JH : (h + 1) * JH], lhsT=wb_w[:, cols].bitcast(E5M2), lhsT_scale=wb_s[:, cols],
+                    p_ps[h, t][:], lhsT=wb_w[:, cols].bitcast(E5M2), lhsT_scale=wb_s[:].bitcast(U8)[:, cols],
                     rhs=hq[h][:].bitcast(E4M3), rhs_scale=hs[h][:], start=True, stop=True,
                 )
         for h in range(H):
@@ -183,14 +187,21 @@ def tile_list_outcomechain_crossed_kernel(
                 cols = slice(t * P, (t + 1) * P)
                 nc.tensor.matmul_mx(
                     q_ps[:, t, h * JH : (h + 1) * JH],
-                    lhsT=wc_w[:, 2 * t * P : 2 * (t + 1) * P].bitcast(E2M1), lhsT_scale=wc_s[:, cols],
+                    lhsT=wc_w[:, 2 * t * P : 2 * (t + 1) * P].bitcast(E2M1), lhsT_scale=wc_s[:].bitcast(U8)[:, cols],
                     rhs=hq[h][:].bitcast(E4M3), rhs_scale=hs[h][:], start=True, stop=True,
                 )
-        p_sb = [tile(f"p_sb{t}", [P, J], F32) for t in range(NT)]
-        nc.scalar.copy(p_sb[0][:], p_ps[0][:])
-        nc.vector.tensor_copy(p_sb[1][:], p_ps[1][:])
-        nc.vector.tensor_copy(pw[0][:].indirect(l3[:]), p_sb[0][:])
-        nc.scalar.activation(pw[1][:].indirect(l3[:]), p_sb[1][:], COPY)
+        p00 = tile("p00", [P, JH], F32)
+        nc.scalar.copy(p00[:], p_ps[0, 0][:])
+        nc.scalar.activation(pw[0][:].indirect(half(l3, 0)), p00[:], COPY)
+        p01 = tile("p01", [P, JH], F32, tag="hid1")
+        nc.vector.tensor_copy(p01[:], p_ps[0, 1][:])
+        nc.vector.tensor_copy(pw[1][:].indirect(half(l3, 0)), p01[:])
+        p10 = tile("p10", [P, JH], F32)
+        p11 = tile("p11", [P, JH], F32)
+        nc.scalar.copy(p10[:], p_ps[1, 0][:])
+        nc.scalar.copy(p11[:], p_ps[1, 1][:])
+        nc.scalar.activation(pw[0][:].indirect(half(l3, 1)), p10[:], COPY)
+        nc.vector.tensor_copy(pw[1][:].indirect(half(l3, 1)), p11[:])
 
         m0 = [tile(f"m0{t}", [P, J], F32) for t in range(NT)]
         g5 = [tile(f"g5{t}", [P, O], F32) for t in range(NT)]

@@ -48,14 +48,12 @@ def tile_list_outcomechain_crossed_kernel(
 
         xo_s = tile("xo_s", [P, Z // 4], I32)
         xt_s = tile("xt_s", [P, T // 4], I32)
-        w_st = tile("w_st", [4, 4, R // 4], I32)
-        w_s = tile("w_s", [P, R // 4], I32)
-        w2_s = tile("w2_s", [P, 4, R // 4], I32)
+        ww_st = tile("ww_st", [4, 4, 2 * R // 4], I32)
+        ww_s = tile("ww_s", [P, 2 * R // 4], I32)
         wb_s = tile("wb_s", [P, N // 4], I32)
         wc_s = tile("wc_s", [P, N // 4], I32)
         nc.vector.memset(xt_s[:], 0)
-        nc.vector.memset(w_s[:], 0)
-        nc.vector.memset(w2_s[:, 0, :], 0)
+        nc.vector.memset(ww_s[:], 0)
         nc.vector.memset(xo_s[:], 0)
         nc.vector.memset(wb_s[:], 0)
         nc.vector.memset(wc_s[:], 0)
@@ -79,12 +77,12 @@ def tile_list_outcomechain_crossed_kernel(
         def load_staged(dst, src):
             nc.sync.dma_start(dst, src[0].rearrange("(q r) n -> r q n", r=4).bitcast(I32))
 
-        load_staged(w_st[:], w_scales)
-        l1 = load_list("l1", offs)
+        load_staged(ww_st[:, :, 0 : R // 4], w_scales)
+        load_staged(ww_st[:, :, R // 4 : 2 * R // 4], w2_scales)
         nc.sync.dma_start(xt_w[:].bitcast(I32), words32(xt_words))
         nc.sync.dma_start(w_w[:].bitcast(I32), words32(w_words))
         load_rows(xt_s, xt_scales)
-        load_staged(w2_s[0:4, :, :], w2_scales)
+        l1 = load_list("l1", offs)
         nc.sync.dma_start(w2_w[:].bitcast(I32), words32(w2_words))
         nc.sync.dma_start(xo_w[:].bitcast(I32), xo_words[0].bitcast(I32))
         l2 = load_list("l2", offs2)
@@ -123,19 +121,18 @@ def tile_list_outcomechain_crossed_kernel(
         w2_d = tile("w2_d", [P, R], U32)
         w_sd = tile("w_sd", [P, R], U8)
         w2_sd = tile("w2_sd", [P, R], U8)
-        deal_words(w_d[:], w_w[:])
-        deal_words(w2_d[:], w2_w[:])
 
         gxo_s, gxo_w, gxt_s, gxt_w = [], [], [], []
-        for q in range(4):
-            nc.vector.tensor_copy(w_s[32 * q : 32 * q + 4, :], w_st[:, q, :])
-        deal_bytes(w_sd[:], w_s[:].bitcast(U8))
+        nc.scalar.copy(ww_s[0:4, :].bitcast(U32), ww_st[:, 0, :].bitcast(U32))
+        for q in range(1, 4):
+            nc.vector.tensor_copy(ww_s[32 * q : 32 * q + 4, :], ww_st[:, q, :])
+        deal_words(w_d[:], w_w[:])
+        deal_words(w2_d[:], w2_w[:])
+        deal_bytes(w_sd[:], ww_s[:, 0 : R // 4].bitcast(U8))
+        deal_bytes(w2_sd[:], ww_s[:, R // 4 : 2 * R // 4].bitcast(U8))
         for h in range(H):
             gxt_w.append(gather_half("gxt_w", xt_w[:], l1, h, U32))
             gxt_s.append(gather_half("gxt_s", xt_s[:].bitcast(U8), l1, h, U8))
-        for q in range(1, 4):
-            nc.vector.tensor_copy(w2_s[32 * q : 32 * q + 4, 0, :], w2_s[0:4, q, :])
-        deal_bytes(w2_sd[:], w2_s[:, 0, :].bitcast(U8))
         for h in range(H):
             gxo_w.append(gather_half("gxo_w", xo_w[:], l2, h, U16))
             gxo_s.append(gather_half("gxo_s", xo_s[:].bitcast(U8), l2, h, U8))

@@ -79,10 +79,10 @@ def tile_list_outcomechain_crossed_kernel(
 
         load_staged(ww_st[:, :, 0 : R // 4], w_scales)
         load_staged(ww_st[:, :, R // 4 : 2 * R // 4], w2_scales)
-        nc.sync.dma_start(xt_w[:].bitcast(I32), words32(xt_words))
-        nc.sync.dma_start(w_w[:].bitcast(I32), words32(w_words))
-        load_rows(xt_s, xt_scales)
         l1 = load_list("l1", offs)
+        nc.sync.dma_start(xt_w[:].bitcast(I32), words32(xt_words))
+        load_rows(xt_s, xt_scales)
+        nc.sync.dma_start(w_w[:].bitcast(I32), words32(w_words))
         nc.sync.dma_start(w2_w[:].bitcast(I32), words32(w2_words))
         nc.sync.dma_start(xo_w[:].bitcast(I32), xo_words[0].bitcast(I32))
         l2 = load_list("l2", offs2)
@@ -123,16 +123,15 @@ def tile_list_outcomechain_crossed_kernel(
         w2_sd = tile("w2_sd", [P, R], U8)
 
         gxo_s, gxo_w, gxt_s, gxt_w = [], [], [], []
-        nc.scalar.copy(ww_s[0:4, :].bitcast(U32), ww_st[:, 0, :].bitcast(U32))
-        for q in range(1, 4):
+        for q in range(4):
             nc.vector.tensor_copy(ww_s[32 * q : 32 * q + 4, :], ww_st[:, q, :])
         deal_words(w_d[:], w_w[:])
         deal_words(w2_d[:], w2_w[:])
         deal_bytes(w_sd[:], ww_s[:, 0 : R // 4].bitcast(U8))
-        deal_bytes(w2_sd[:], ww_s[:, R // 4 : 2 * R // 4].bitcast(U8))
         for h in range(H):
             gxt_w.append(gather_half("gxt_w", xt_w[:], l1, h, U32))
             gxt_s.append(gather_half("gxt_s", xt_s[:].bitcast(U8), l1, h, U8))
+        deal_bytes(w2_sd[:], ww_s[:, R // 4 : 2 * R // 4].bitcast(U8))
         for h in range(H):
             gxo_w.append(gather_half("gxo_w", xo_w[:], l2, h, U16))
             gxo_s.append(gather_half("gxo_s", xo_s[:].bitcast(U8), l2, h, U8))
@@ -187,18 +186,13 @@ def tile_list_outcomechain_crossed_kernel(
                     lhsT=wc_w[:, 2 * t * P : 2 * (t + 1) * P].bitcast(E2M1), lhsT_scale=wc_s[:].bitcast(U8)[:, cols],
                     rhs=hq[h][:].bitcast(E4M3), rhs_scale=hs[h][:], start=True, stop=True,
                 )
-        p00 = tile("p00", [P, JH], F32)
-        nc.scalar.copy(p00[:], p_ps[0, 0][:])
-        nc.scalar.activation(pw[0][:].indirect(half(l3, 0)), p00[:], COPY)
-        p01 = tile("p01", [P, JH], F32, tag="hid1")
-        nc.vector.tensor_copy(p01[:], p_ps[0, 1][:])
-        nc.vector.tensor_copy(pw[1][:].indirect(half(l3, 0)), p01[:])
-        p10 = tile("p10", [P, JH], F32)
-        p11 = tile("p11", [P, JH], F32)
-        nc.scalar.copy(p10[:], p_ps[1, 0][:])
-        nc.scalar.copy(p11[:], p_ps[1, 1][:])
-        nc.scalar.activation(pw[0][:].indirect(half(l3, 1)), p10[:], COPY)
-        nc.vector.tensor_copy(pw[1][:].indirect(half(l3, 1)), p11[:])
+        for h in range(H):
+            p_for_scalar = tile(f"p{h}0_sb", [P, JH], F32)
+            p_for_vector = tile(f"p{h}1_sb", [P, JH], F32, tag="a_sb11" if h == 0 else None)
+            nc.vector.tensor_copy(p_for_scalar[:], p_ps[h, 0][:])
+            nc.scalar.copy(p_for_vector[:], p_ps[h, 1][:])
+            nc.scalar.activation(pw[0][:].indirect(half(l3, h)), p_for_scalar[:], COPY)
+            nc.vector.tensor_copy(pw[1][:].indirect(half(l3, h)), p_for_vector[:])
 
         m0 = [tile(f"m0{t}", [P, J], F32) for t in range(NT)]
         g5 = [tile(f"g5{t}", [P, O], F32) for t in range(NT)]

from contextlib import ExitStack

import concourse.mybir as mybir

K, T, Z, J, R, N, C, O = 512, 1024, 1024, 256, 512, 256, 512, 128
FLOPS = 2 * (4 * K * R * J + 2 * R * N * J)

F32 = mybir.dt.float32
BF16 = mybir.dt.bfloat16
I32 = mybir.dt.int32
U32 = mybir.dt.uint32
U16 = mybir.dt.uint16
U8 = mybir.dt.uint8
E4M3 = mybir.dt.float8_e4m3fn_x4
E5M2 = mybir.dt.float8_e5m2_x4
E2M1 = mybir.dt.float4_e2m1fn_x4
COPY = mybir.ActivationFunctionType.Copy
MAX = mybir.AluOpType.max
SUB = mybir.AluOpType.subtract

P = 128
PACK = 4
H = 2
JH = J // H
NT = N // P


def tile_list_outcomechain_crossed_kernel(
    tc, xt_words, xt_scales, xo_words, xo_scales, w_words, w_scales, w2_words, w2_scales,
    wb_words, wb_scales, wc_words, wc_scales, so, sp, offs, offs2, offs3, offs4, offs5, offs6, out,
):
    nc = tc.nc
    with ExitStack() as ctx:
        lists = ctx.enter_context(tc.tile_pool(name="lists", bufs=1))
        sb = ctx.enter_context(tc.tile_pool(name="sb", bufs=1))
        ps = ctx.enter_context(tc.psum_pool(name="ps", bufs=1))

        def tile(name, shape, dtype, tag=None):
            return sb.tile(shape, dtype, name=name, tag=tag or name, align_bytes=64)

        def load_list(name, src):
            t = lists.tile(list(src.shape), U16, name=name)
            nc.sync.dma_start(t[:], src)
            return t

        def words32(src):
            return src[0].rearrange("p n t -> p (n t)").bitcast(I32)

        xo_s = tile("xo_s", [P, Z // 4], I32)
        xt_s = tile("xt_s", [P, T // 4], I32)
        ww_st = tile("ww_st", [4, 4, 2 * R // 4], I32)
        ww_s = tile("ww_s", [P, 2 * R // 4], I32)
        wb_s = tile("wb_s", [P, N // 4], I32)
        wc_s = tile("wc_s", [P, N // 4], I32)
        nc.vector.memset(xt_s[:], 0)
        nc.vector.memset(ww_s[:], 0)
        nc.vector.memset(xo_s[:], 0)
        nc.vector.memset(wb_s[:], 0)
        nc.vector.memset(wc_s[:], 0)
        pw = [tile(f"pw{t}", [P, C], F32) for t in range(NT)]
        for t in range(NT):
            nc.vector.memset(pw[t][:], 0.0)

        xo_w = tile("xo_w", [P, Z], U16)
        xt_w = tile("xt_w", [P, T], U32)
        w_w = tile("w_w", [P, R], U32)
        w2_w = tile("w2_w", [P, R], U32)
        wb_w = tile("wb_w", [P, N], U32)
        wc_w = tile("wc_w", [P, 2 * N], U8)
        so_t = tile("so_t", [P, NT], F32)
        sp_t = tile("sp_t", [P, NT], F32)

        def load_rows(plane, src):
            for q in range(4):
                nc.sync.dma_start(plane[32 * q : 32 * q + 4, :], src[0, 4 * q : 4 * q + 4, :].bitcast(I32))

        def load_staged(dst, src):
            nc.sync.dma_start(dst, src[0].rearrange("(q r) n -> r q n", r=4).bitcast(I32))

        load_staged(ww_st[:, :, 0 : R // 4], w_scales)
        load_staged(ww_st[:, :, R // 4 : 2 * R // 4], w2_scales)
        l1 = load_list("l1", offs)
        nc.sync.dma_start(xt_w[:].bitcast(I32), words32(xt_words))
        load_rows(xt_s, xt_scales)
        nc.sync.dma_start(w_w[:].bitcast(I32), words32(w_words))
        nc.sync.dma_start(w2_w[:].bitcast(I32), words32(w2_words))
        nc.sync.dma_start(xo_w[:].bitcast(I32), xo_words[0].bitcast(I32))
        l2 = load_list("l2", offs2)
        load_rows(xo_s, xo_scales)
        load_rows(wb_s, wb_scales)
        nc.sync.dma_start(wb_w[:].bitcast(I32), words32(wb_words))
        l3 = load_list("l3", offs3)
        nc.sync.dma_start(wc_w[:].bitcast(I32), wc_words[0].bitcast(I32))
        load_rows(wc_s, wc_scales)
        l4 = load_list("l4", offs4)
        with nc.allow_non_contiguous_dma(reason="one value a partition"):
            nc.sync.dma_start(so_t[:], so.rearrange("(t p) o -> p (t o)", p=P))
            nc.sync.dma_start(sp_t[:], sp.rearrange("(t p) o -> p (t o)", p=P))
        l6 = load_list("l6", offs6)
        l5 = load_list("l5", offs5)


        def deal_words(dst, src):
            nc.scalar.copy(
                dst.rearrange("p (t m i) -> p m t i", t=PACK, i=4), src.rearrange("p (m i t) -> p m t i", t=PACK, i=4)
            )

        def deal_bytes(dst, src):
            nc.vector.tensor_copy(dst.rearrange("p (t m) -> p t m", t=PACK), src.rearrange("p (m t) -> p t m", t=PACK))

        def half(lst, h):
            cols = JH // 16
            return lst[:, h * cols : (h + 1) * cols]

        def gather_half(name, window, lst, h, dtype):
            g = tile(f"{name}{h}", [P, JH], dtype)
            nc.vector.tensor_copy(g[:], window.indirect(half(lst, h)))
            return g

        w_d = tile("w_d", [P, R], U32)
        w2_d = tile("w2_d", [P, R], U32)
        w_sd = tile("w_sd", [P, R], U8)
        w2_sd = tile("w2_sd", [P, R], U8)

        gxo_s, gxo_w, gxt_s, gxt_w = [], [], [], []
        for q in range(4):
            nc.vector.tensor_copy(ww_s[32 * q : 32 * q + 4, :], ww_st[:, q, :])
        deal_words(w_d[:], w_w[:])
        deal_words(w2_d[:], w2_w[:])
        deal_bytes(w_sd[:], ww_s[:, 0 : R // 4].bitcast(U8))
        for h in range(H):
            gxt_w.append(gather_half("gxt_w", xt_w[:], l1, h, U32))
            gxt_s.append(gather_half("gxt_s", xt_s[:].bitcast(U8), l1, h, U8))
        deal_bytes(w2_sd[:], ww_s[:, R // 4 : 2 * R // 4].bitcast(U8))
        for h in range(H):
            gxo_w.append(gather_half("gxo_w", xo_w[:], l2, h, U16))
            gxo_s.append(gather_half("gxo_s", xo_s[:].bitcast(U8), l2, h, U8))

        a_ps = [ps.tile([P, PACK, JH], F32, name=f"a{h}") for h in range(H)]
        b_ps = [ps.tile([P, PACK, JH], F32, name=f"b{h}") for h in range(H)]

        def passes(bank, words, scales, x_words, x_scales, first):
            for t in range(PACK):
                cols = slice(t * P, (t + 1) * P)
                nc.tensor.matmul_mx(
                    bank[:, t, :], lhsT=words[:, cols].bitcast(E5M2), lhsT_scale=scales[:, cols],
                    rhs=x_words, rhs_scale=x_scales,
                    start=first and t == 0, stop=(not first) and t == PACK - 1,
                )

        for h in range(H):
            passes(a_ps[h], w_d, w_sd, gxt_w[h][:].bitcast(E4M3), gxt_s[h][:], True)
        for h in range(H):
            passes(b_ps[h], w2_d, w2_sd, gxt_w[h][:].bitcast(E4M3), gxt_s[h][:], True)
        for h in range(H):
            passes(a_ps[h], w2_d, w2_sd, gxo_w[h][:].bitcast(E2M1), gxo_s[h][:], False)
            passes(b_ps[h], w_d, w_sd, gxo_w[h][:].bitcast(E2M1), gxo_s[h][:], False)

        q_ps = ps.tile([P, NT, J], F32, name="q")
        JQ = JH // 2
        hq, hs = [], []
        for h in range(H):
            hid = tile(f"hid{h}", [P, JH, PACK], BF16)
            for u in range(2):
                js = slice(u * JQ, (u + 1) * JQ)
                a_sb = tile(f"a_sb{h}{u}", [P, JQ, PACK], F32)
                nc.scalar.activation(a_sb[:], a_ps[h][:, :, js].rearrange("p t j -> p j t"), COPY)
                nc.vector.tensor_tensor(hid[:, js, :], b_ps[h][:, :, js].rearrange("p t j -> p j t"), a_sb[:], MAX)
            hq.append(tile(f"hq{h}", [P, JH], U32))
            hs.append(tile(f"hs{h}", [P, JH], U8))
            nc.vector.quantize_mx(hq[h][:].bitcast(E4M3), hs[h][:], hid[:].rearrange("p j t -> p (j t)"))
        p_ps = {}
        for h in range(H):
            for t in range(NT):
                cols = slice(t * P, (t + 1) * P)
                p_ps[h, t] = ps.tile([P, JH], F32, name=f"p{h}{t}", tag="a0" if (h, t) == (1, 1) else f"p{h}{t}")
                nc.tensor.matmul_mx(
                    p_ps[h, t][:], lhsT=wb_w[:, cols].bitcast(E5M2), lhsT_scale=wb_s[:].bitcast(U8)[:, cols],
                    rhs=hq[h][:].bitcast(E4M3), rhs_scale=hs[h][:], start=True, stop=True,
                )
        for h in range(H):
            for t in range(NT):
                cols = slice(t * P, (t + 1) * P)
                nc.tensor.matmul_mx(
                    q_ps[:, t, h * JH : (h + 1) * JH],
                    lhsT=wc_w[:, 2 * t * P : 2 * (t + 1) * P].bitcast(E2M1), lhsT_scale=wc_s[:].bitcast(U8)[:, cols],
                    rhs=hq[h][:].bitcast(E4M3), rhs_scale=hs[h][:], start=True, stop=True,
                )
        for h in range(H):
            p_for_scalar = tile(f"p{h}0_sb", [P, JH], F32)
            p_for_vector = tile(f"p{h}1_sb", [P, JH], F32, tag="a_sb11" if h == 0 else None)
            nc.vector.tensor_copy(p_for_scalar[:], p_ps[h, 0][:])
            nc.scalar.copy(p_for_vector[:], p_ps[h, 1][:])
            nc.scalar.activation(pw[0][:].indirect(half(l3, h)), p_for_scalar[:], COPY)
            nc.vector.tensor_copy(pw[1][:].indirect(half(l3, h)), p_for_vector[:])

        m0 = [tile(f"m0{t}", [P, J], F32) for t in range(NT)]
        g5 = [tile(f"g5{t}", [P, O], F32) for t in range(NT)]
        for t in range(NT):
            for h in range(H):
                js = slice(h * JH, (h + 1) * JH)
                g4 = tile(f"g4{t}{h}", [P, JH], F32)
                nc.scalar.activation(g4[:], pw[t][:].indirect(half(l4, h)), COPY, scale=so_t[:, t : t + 1])
                nc.vector.tensor_tensor(m0[t][:, js], q_ps[:, t, js], g4[:], MAX)
            nc.vector.tensor_copy(g5[t][:], m0[t][:].indirect(l5[:]))
        for t in range(NT):
            g6 = tile(f"g6{t}", [P, O], F32)
            nc.scalar.activation(g6[:], m0[t][:].indirect(l6[:]), COPY, scale=sp_t[:, t : t + 1])
            y = tile(f"y{t}", [P, O], F32)
            nc.vector.tensor_tensor(y[:], g5[t][:], g6[:], SUB)
            nc.sync.dma_start(out[t * P : (t + 1) * P, :], y[:])
